import numpy as np
import ml_dtypes


def mxq(x, axis, fmt="e4m3"):
    dtype, down = {"e4m3": (ml_dtypes.float8_e4m3fn, 7), "e5m2": (ml_dtypes.float8_e5m2, 14)}[fmt]
    v = np.moveaxis(np.asarray(x, np.float32).astype(ml_dtypes.bfloat16).astype(np.float64), axis, -1)
    blocks = v.reshape(v.shape[:-1] + (-1, 32))
    amax = np.abs(blocks).max(-1, keepdims=True)
    byte = np.maximum(np.where(amax > 0, np.frexp(amax)[1] - 1 + 127, 0) - down, 1)
    scale = np.exp2(byte - 127.0)
    codes = (blocks / scale).astype(np.float32).astype(dtype).astype(np.float64)
    return np.moveaxis((codes * scale).reshape(v.shape), -1, axis)


WIDE = False


def mx_kscale(k):
    if not WIDE:
        return np.ones(k)
    levels = np.array([10, -10, 5, -5, 0])
    if k % 512:
        return np.exp2(np.random.permutation(np.resize(levels, k // 32))).repeat(32)
    a = np.empty((k // 512, 16))
    for p in range(k // 512):
        a[p, :8] = np.random.permutation(np.resize(levels, 8))
        for g in range(8):
            far = levels[np.abs(levels - a[p, g]) >= 10]
            a[p, g + 8] = far[np.random.randint(len(far))]
    return np.exp2(a.ravel()).repeat(32)


def f64(x):
    return np.asarray(x).astype(np.float64)


def striped(idx):
    return np.tile(idx.reshape(-1, 16).T, (8, 1)).astype(np.uint16)


def unstriped(offs):
    return offs[:16].T.reshape(-1).astype(np.int64)


def pack_weight(w):
    k, n = w.shape
    w = f64(np.asarray(w, np.float32).astype(ml_dtypes.bfloat16)).reshape(k // 32, 32, n)
    amax = np.abs(w).max(1)
    byte = np.clip(np.where(amax > 0, np.frexp(amax)[1] - 1 + 127 - 7, 1), 1, 254)
    scaled = (w * np.exp2(127.0 - byte)[:, None, :]).reshape(k, n).astype(np.float32)
    words = np.ascontiguousarray(scaled.reshape(k // 512, 128, 4, n).transpose(0, 1, 3, 2)).astype(ml_dtypes.float8_e4m3fn).view(np.uint8)
    return words, np.ascontiguousarray(byte.astype(np.uint8).reshape(k // 512, 16, n))


def unpack_weight(words, scales):
    g, p, n, _ = words.shape
    vals = np.ascontiguousarray(words).view(ml_dtypes.float8_e4m3fn).astype(np.float64) * np.repeat(np.exp2(scales.astype(np.float64) - 127.0), 8, axis=1)[..., None]
    return vals.transpose(0, 1, 3, 2).reshape(g * 512, n)


def sigmoid(v):
    return 1.0 / (1.0 + np.exp(-np.maximum(v, -700.0)))


K, T, S, V, N = 1024, 2048, 512, 256, 128


def setup_inputs():
    n = np.random.standard_normal
    s = mx_kscale(K)[:, None]
    packed_xT = pack_weight(n((K, T)) * s)
    return {
        "x_words": packed_xT[0],
        "x_scales": packed_xT[1],
        "w1": (n((K, N)) / np.sqrt(K) / s).astype(np.float32),
        "w2": (n((K, N)) / np.sqrt(K) / s).astype(np.float32),
        "w3": (n((K, N)) / np.sqrt(K) / s).astype(np.float32),
        "offs": striped(np.random.permutation(T)[:S]),
        "cen": striped(np.random.permutation(S)[:V]),
        "pos1": striped(np.random.permutation(S)[:V]),
        "pos2": striped(np.random.permutation(S)[:V]),
        "pos3": striped(np.random.permutation(S)[:V]),
    }


def reference(x_words, x_scales, w1, w2, w3, offs, cen, pos1, pos2, pos3):
    xq = unpack_weight(x_words, x_scales)[:, unstriped(offs)]
    y = mxq(f64(w1), 0, "e4m3").T @ xq
    yc = y[:, unstriped(cen)]
    e = mxq(f64(w2), 0, "e4m3").T @ xq
    h = mxq(f64(w3), 0, "e4m3").T @ xq
    z = (sigmoid(yc + e[:, unstriped(pos1)])) * h[:, unstriped(pos1)] + (sigmoid(yc + e[:, unstriped(pos2)])) * h[:, unstriped(pos2)] + (sigmoid(yc + e[:, unstriped(pos3)])) * h[:, unstriped(pos3)]
    return z

@@ -1,0 +1,152 @@
+from contextlib import ExitStack
+
+import concourse.mybir as mybir
+
+K, T, S, V, N = 1024, 2048, 512, 256, 128
+FLOPS = 3 * 2 * K * S * N
+
+F32 = mybir.dt.float32
+BF16 = mybir.dt.bfloat16
+I32 = mybir.dt.int32
+U32 = mybir.dt.uint32
+U16 = mybir.dt.uint16
+U8 = mybir.dt.uint8
+FP8X4 = mybir.dt.float8_e4m3fn_x4
+ADD = mybir.AluOpType.add
+MULT = mybir.AluOpType.mult
+SIGMOID = mybir.ActivationFunctionType.Sigmoid
+
+P = 128
+PACK = 4
+K_PASS = P * PACK
+PASSES = K // K_PASS
+HALF = S // 2
+PER_COL = 16
+
+
+def tile_picked_gatedg_none_p_kernel(tc, x_words, x_scales, w1, w2, w3, offs, cen, pos1, pos2, pos3, out):
+    nc = tc.nc
+    with ExitStack() as ctx:
+        keep = ctx.enter_context(tc.tile_pool(name="keep", bufs=1))
+        psum = ctx.enter_context(tc.psum_pool(name="psum", bufs=1))
+
+        def load_list(name, src):
+            t = keep.tile(list(src.shape), U16, name=name)
+            nc.sync.dma_start(t[:], src)
+            return t
+
+        def load_words(z):
+            t = keep.tile([P, T], I32, name=f"x_table{z}")
+            nc.sync.dma_start(t[:], x_words[z].rearrange("p n t -> p (n t)").bitcast(I32))
+            return t
+
+        def load_weight(name, w, z):
+            t = keep.tile([P, PACK, N], F32, name=f"{name}_raw{z}", tag=f"{name}_wide{z}")
+            nc.sync.dma_start(t[:], w[z * K_PASS : (z + 1) * K_PASS, :].rearrange("(p j) n -> p j n", j=PACK))
+            return t
+
+        scale_table = keep.tile([P, T], U8, name="scale_table")
+        nc.vector.memset(scale_table[:].bitcast(I32), 0)
+        warm = keep.tile([P, 2], F32, name="warm")
+        nc.vector.memset(warm[:, 0:1], 0.0)
+        nc.scalar.activation(warm[:, 1:2], warm[:, 0:1], SIGMOID)
+
+        table = [None, None]
+        table[0] = load_words(0)
+        for q in range(4):
+            nc.sync.dma_start(
+                scale_table[32 * q : 32 * q + 4 * PASSES, :].bitcast(I32),
+                x_scales[:, 4 * q : 4 * q + 4, :].bitcast(I32),
+            )
+
+        offs_t = load_list("offs_t", offs)
+        raw = {}
+        raw["e"] = [load_weight("e", w2, z) for z in range(PASSES)]
+        table[1] = load_words(1)
+        pos_t = [load_list("pos1_t", pos1)]
+        raw["y"] = [load_weight("y", w1, z) for z in range(PASSES)]
+        pos_t.append(load_list("pos2_t", pos2))
+        pos_t.append(load_list("pos3_t", pos3))
+        cen_t = load_list("cen_t", cen)
+        raw["h"] = [load_weight("h", w3, z) for z in range(PASSES)]
+
+        def quantize(name, z):
+            g = keep.tile([P, N, PACK], BF16, name=f"{name}_bf{z}", tag=f"{name}_stage{z}", align_bytes=64)
+            nc.scalar.copy(
+                g[:].rearrange("p (c i) t -> p c t i", i=4),
+                raw[name][z][:].rearrange("p t (c i) -> p c t i", i=4),
+            )
+            codes = keep.tile([P, N], U32, name=f"{name}_codes{z}", align_bytes=64)
+            scales = keep.tile([P, N], U8, name=f"{name}_scales{z}", align_bytes=64)
+            nc.vector.quantize_mx(out=codes[:].bitcast(FP8X4), scales=scales[:], in_=g[:].rearrange("p n t -> p (n t)"))
+            return codes, scales
+
+        x_codes = [[keep.tile([P, HALF], U32, name=f"x_codes{z}_{u}", align_bytes=64) for u in range(2)] for z in range(PASSES)]
+        x_sc = keep.tile([P, S], U8, name="x_sc", align_bytes=64)
+
+        def gather_words(z, u):
+            o = offs_t[:, u * HALF // PER_COL : (u + 1) * HALF // PER_COL]
+            nc.vector.tensor_copy(x_codes[z][u][:], table[z][:].bitcast(U32).indirect(o))
+
+        banks = {}
+
+        def product(name, wq, z, u):
+            if z == 0:
+                banks[name, u] = psum.tile([P, HALF], F32, name=f"{name}_acc{u}")
+            nc.tensor.matmul_mx(
+                out=banks[name, u][:],
+                lhsT=wq[0][:].bitcast(FP8X4),
+                lhsT_scale=wq[1][:],
+                rhs=x_codes[z][u][:].bitcast(FP8X4),
+                rhs_scale=x_sc[4 * z : P, u * HALF : (u + 1) * HALF],
+                start=(z == 0),
+                stop=(z == PASSES - 1),
+            )
+
+        res = {"e": keep.tile([P, S], F32, name="e_rows")}
+
+        gather_words(0, 0)
+        gather_words(0, 1)
+        wq = {("e", z): quantize("e", z) for z in range(PASSES)}
+        nc.vector.tensor_copy(x_sc[:], scale_table[:].indirect(offs_t[:]))
+        for u in range(2):
+            product("e", wq["e", 0], 0, u)
+        for u in range(2):
+            gather_words(1, u)
+            product("e", wq["e", 1], 1, u)
+        nc.scalar.copy(res["e"][:, 0:HALF], banks["e", 0][:])
+        nc.vector.tensor_copy(res["e"][:, HALF:S], banks["e", 1][:])
+
+        for name in ("y", "h"):
+            for z in range(PASSES):
+                wq[name, z] = quantize(name, z)
+                for u in range(2):
+                    product(name, wq[name, z], z, u)
+        res["y"] = keep.tile([P, S], F32, name="y_rows", tag="h_wide1")
+        res["h"] = keep.tile([P, S], F32, name="h_rows")
+        for name in ("y", "h"):
+            for u in range(2):
+                nc.scalar.copy(res[name][:, u * HALF : (u + 1) * HALF], banks[name, u][:])
+
+        reuse = ("y_stage1", "h_stage0", "h_stage1")
+        e_g = [keep.tile([P, V], F32, name=f"e_g{d}", tag=reuse[d], align_bytes=64) for d in range(3)]
+        for d in range(3):
+            nc.vector.tensor_copy(e_g[d][:], res["e"][:].indirect(pos_t[d][:]))
+        yc = keep.tile([P, V], F32, name="yc")
+        nc.vector.tensor_copy(yc[:], res["y"][:].indirect(cen_t[:]))
+        gate = []
+        for d in range(3):
+            pre = keep.tile([P, V], F32, name=f"pre{d}")
+            nc.vector.tensor_tensor(pre[:], e_g[d][:], yc[:], ADD)
+            g = keep.tile([P, V], F32, name=f"gate{d}")
+            nc.scalar.activation(g[:], pre[:], SIGMOID)
+            gate.append(g)
+        term = [keep.tile([P, V], F32, name=f"term{d}") for d in range(3)]
+        nc.vector.tensor_tensor(term[0][:], res["h"][:].indirect(pos_t[0][:]), gate[0][:], MULT)
+        nc.vector.tensor_tensor(term[1][:], res["h"][:].indirect(pos_t[1][:]), gate[1][:], MULT)
+        nc.vector.tensor_tensor(term[2][:], res["h"][:].indirect(pos_t[2][:]), gate[2][:], MULT)
+        part = keep.tile([P, V], F32, name="part")
+        nc.vector.tensor_tensor(part[:], term[0][:], term[1][:], ADD)
+        total = keep.tile([P, V], F32, name="total")
+        nc.vector.tensor_tensor(total[:], part[:], term[2][:], ADD)
+        nc.sync.dma_start(out, total[:])

@@ -61,21 +61,24 @@ def tile_picked_gatedg_none_p_kernel(tc, x_words, x_scales, w1, w2, w3, offs, ce
 
         offs_t = load_list("offs_t", offs)
         raw = {}
-        raw["e"] = [load_weight("e", w2, z) for z in range(PASSES)]
+        y_raw = keep.tile([P, PASSES, PACK * N], F32, name="y_raw")
+        nc.sync.dma_start(y_raw[:], w1.rearrange("(z p j) n -> p z (j n)", z=PASSES, j=PACK))
+        raw["y"] = [y_raw[:, z, :].rearrange("p (j n) -> p j n", j=PACK) for z in range(PASSES)]
         table[1] = load_words(1)
-        pos_t = [load_list("pos1_t", pos1)]
-        raw["y"] = [load_weight("y", w1, z) for z in range(PASSES)]
-        pos_t.append(load_list("pos2_t", pos2))
-        pos_t.append(load_list("pos3_t", pos3))
+        raw["e"] = [load_weight("e", w2, z)[:] for z in range(PASSES)]
         cen_t = load_list("cen_t", cen)
-        raw["h"] = [load_weight("h", w3, z) for z in range(PASSES)]
+        raw["h"] = [load_weight("h", w3, z)[:] for z in range(PASSES)]
+        pos_t = [load_list(f"pos{d + 1}_t", pos) for d, pos in enumerate((pos1, pos2, pos3))]
 
         def quantize(name, z):
             g = keep.tile([P, N, PACK], BF16, name=f"{name}_bf{z}", tag=f"{name}_stage{z}", align_bytes=64)
-            nc.scalar.copy(
-                g[:].rearrange("p (c i) t -> p c t i", i=4),
-                raw[name][z][:].rearrange("p t (c i) -> p c t i", i=4),
-            )
+            if (name, z) == ("e", 1):
+                nc.vector.tensor_copy(
+                    g[:].rearrange("p (c i) t -> p c t i", i=4),
+                    raw[name][z].rearrange("p t (c i) -> p c t i", i=4),
+                )
+            else:
+                nc.scalar.copy(g[:], raw[name][z].rearrange("p t n -> p n t"))
             codes = keep.tile([P, N], U32, name=f"{name}_codes{z}", align_bytes=64)
             scales = keep.tile([P, N], U8, name=f"{name}_scales{z}", align_bytes=64)
             nc.vector.quantize_mx(out=codes[:].bitcast(FP8X4), scales=scales[:], in_=g[:].rearrange("p n t -> p (n t)"))
@@ -103,41 +106,38 @@ def tile_picked_gatedg_none_p_kernel(tc, x_words, x_scales, w1, w2, w3, offs, ce
                 stop=(z == PASSES - 1),
             )
 
-        res = {"e": keep.tile([P, S], F32, name="e_rows")}
+        res = {}
 
         gather_words(0, 0)
         gather_words(0, 1)
-        wq = {("e", z): quantize("e", z) for z in range(PASSES)}
+        wq = {("y", z): quantize("y", z) for z in range(PASSES)}
         nc.vector.tensor_copy(x_sc[:], scale_table[:].indirect(offs_t[:]))
         for u in range(2):
-            product("e", wq["e", 0], 0, u)
+            product("y", wq["y", 0], 0, u)
         for u in range(2):
             gather_words(1, u)
-            product("e", wq["e", 1], 1, u)
-        nc.scalar.copy(res["e"][:, 0:HALF], banks["e", 0][:])
-        nc.vector.tensor_copy(res["e"][:, HALF:S], banks["e", 1][:])
+            product("y", wq["y", 1], 1, u)
 
-        for name in ("y", "h"):
+        for name in ("e", "h"):
             for z in range(PASSES):
                 wq[name, z] = quantize(name, z)
                 for u in range(2):
                     product(name, wq[name, z], z, u)
-        res["y"] = keep.tile([P, S], F32, name="y_rows", tag="h_wide1")
+        res["y"] = keep.tile([P, S], F32, name="y_rows", tag="e_stage1", align_bytes=64)
+        for u in range(2):
+            nc.vector.tensor_copy(res["y"][:, u * HALF : (u + 1) * HALF], banks["y", u][:])
+        res["e"] = keep.tile([P, S], F32, name="e_rows", tag="h_wide0")
         res["h"] = keep.tile([P, S], F32, name="h_rows")
-        for name in ("y", "h"):
+        for name in ("e", "h"):
             for u in range(2):
                 nc.scalar.copy(res[name][:, u * HALF : (u + 1) * HALF], banks[name, u][:])
 
-        reuse = ("y_stage1", "h_stage0", "h_stage1")
-        e_g = [keep.tile([P, V], F32, name=f"e_g{d}", tag=reuse[d], align_bytes=64) for d in range(3)]
-        for d in range(3):
-            nc.vector.tensor_copy(e_g[d][:], res["e"][:].indirect(pos_t[d][:]))
-        yc = keep.tile([P, V], F32, name="yc")
+        yc = keep.tile([P, V], F32, name="yc", tag="h_stage0", align_bytes=64)
         nc.vector.tensor_copy(yc[:], res["y"][:].indirect(cen_t[:]))
         gate = []
         for d in range(3):
-            pre = keep.tile([P, V], F32, name=f"pre{d}")
-            nc.vector.tensor_tensor(pre[:], e_g[d][:], yc[:], ADD)
+            pre = keep.tile([P, V], F32, name=f"pre{d}", tag=("h_stage1", "pre1", "pre2")[d], align_bytes=64)
+            nc.vector.tensor_tensor(pre[:], res["e"][:].indirect(pos_t[d][:]), yc[:], ADD)
             g = keep.tile([P, V], F32, name=f"gate{d}")
             nc.scalar.activation(g[:], pre[:], SIGMOID)
             gate.append(g)

from contextlib import ExitStack

import concourse.mybir as mybir

K, T, S, V, N = 1024, 2048, 512, 256, 128
FLOPS = 3 * 2 * K * S * N

F32 = mybir.dt.float32
BF16 = mybir.dt.bfloat16
I32 = mybir.dt.int32
U32 = mybir.dt.uint32
U16 = mybir.dt.uint16
U8 = mybir.dt.uint8
FP8X4 = mybir.dt.float8_e4m3fn_x4
ADD = mybir.AluOpType.add
MULT = mybir.AluOpType.mult
SIGMOID = mybir.ActivationFunctionType.Sigmoid

P = 128
PACK = 4
K_PASS = P * PACK
PASSES = K // K_PASS
HALF = S // 2
PER_COL = 16


def tile_picked_gatedg_none_p_kernel(tc, x_words, x_scales, w1, w2, w3, offs, cen, pos1, pos2, pos3, out):
    nc = tc.nc
    with ExitStack() as ctx:
        keep = ctx.enter_context(tc.tile_pool(name="keep", bufs=1))
        psum = ctx.enter_context(tc.psum_pool(name="psum", bufs=1))

        def load_list(name, src):
            t = keep.tile(list(src.shape), U16, name=name)
            nc.sync.dma_start(t[:], src)
            return t

        def load_words(z):
            t = keep.tile([P, T], I32, name=f"x_table{z}")
            nc.sync.dma_start(t[:], x_words[z].rearrange("p n t -> p (n t)").bitcast(I32))
            return t

        def load_weight(name, w, z):
            t = keep.tile([P, PACK, N], F32, name=f"{name}_raw{z}", tag=f"{name}_wide{z}")
            nc.sync.dma_start(t[:], w[z * K_PASS : (z + 1) * K_PASS, :].rearrange("(p j) n -> p j n", j=PACK))
            return t

        scale_table = keep.tile([P, T], U8, name="scale_table")
        nc.vector.memset(scale_table[:].bitcast(I32), 0)
        warm = keep.tile([P, 2], F32, name="warm")
        nc.vector.memset(warm[:, 0:1], 0.0)
        nc.scalar.activation(warm[:, 1:2], warm[:, 0:1], SIGMOID)

        table = [None, None]
        table[0] = load_words(0)
        for q in range(4):
            nc.sync.dma_start(
                scale_table[32 * q : 32 * q + 4 * PASSES, :].bitcast(I32),
                x_scales[:, 4 * q : 4 * q + 4, :].bitcast(I32),
            )

        offs_t = load_list("offs_t", offs)
        raw = {}
        y_raw = keep.tile([P, PASSES, PACK * N], F32, name="y_raw")
        nc.sync.dma_start(y_raw[:], w1.rearrange("(z p j) n -> p z (j n)", z=PASSES, j=PACK))
        raw["y"] = [y_raw[:, z, :].rearrange("p (j n) -> p j n", j=PACK) for z in range(PASSES)]
        table[1] = load_words(1)
        raw["e"] = [load_weight("e", w2, z)[:] for z in range(PASSES)]
        cen_t = load_list("cen_t", cen)
        raw["h"] = [load_weight("h", w3, z)[:] for z in range(PASSES)]
        pos_t = [load_list(f"pos{d + 1}_t", pos) for d, pos in enumerate((pos1, pos2, pos3))]

        def quantize(name, z):
            g = keep.tile([P, N, PACK], BF16, name=f"{name}_bf{z}", tag=f"{name}_stage{z}", align_bytes=64)
            if (name, z) == ("e", 1):
                nc.vector.tensor_copy(
                    g[:].rearrange("p (c i) t -> p c t i", i=4),
                    raw[name][z].rearrange("p t (c i) -> p c t i", i=4),
                )
            else:
                nc.scalar.copy(g[:], raw[name][z].rearrange("p t n -> p n t"))
            codes = keep.tile([P, N], U32, name=f"{name}_codes{z}", align_bytes=64)
            scales = keep.tile([P, N], U8, name=f"{name}_scales{z}", align_bytes=64)
            nc.vector.quantize_mx(out=codes[:].bitcast(FP8X4), scales=scales[:], in_=g[:].rearrange("p n t -> p (n t)"))
            return codes, scales

        x_codes = [[keep.tile([P, HALF], U32, name=f"x_codes{z}_{u}", align_bytes=64) for u in range(2)] for z in range(PASSES)]
        x_sc = keep.tile([P, S], U8, name="x_sc", align_bytes=64)

        def gather_words(z, u):
            o = offs_t[:, u * HALF // PER_COL : (u + 1) * HALF // PER_COL]
            nc.vector.tensor_copy(x_codes[z][u][:], table[z][:].bitcast(U32).indirect(o))

        banks = {}

        def product(name, wq, z, u):
            if z == 0:
                banks[name, u] = psum.tile([P, HALF], F32, name=f"{name}_acc{u}")
            nc.tensor.matmul_mx(
                out=banks[name, u][:],
                lhsT=wq[0][:].bitcast(FP8X4),
                lhsT_scale=wq[1][:],
                rhs=x_codes[z][u][:].bitcast(FP8X4),
                rhs_scale=x_sc[4 * z : P, u * HALF : (u + 1) * HALF],
                start=(z == 0),
                stop=(z == PASSES - 1),
            )

        res = {}

        gather_words(0, 0)
        gather_words(0, 1)
        wq = {("y", z): quantize("y", z) for z in range(PASSES)}
        nc.vector.tensor_copy(x_sc[:], scale_table[:].indirect(offs_t[:]))
        for u in range(2):
            product("y", wq["y", 0], 0, u)
        for u in range(2):
            gather_words(1, u)
            product("y", wq["y", 1], 1, u)

        for name in ("e", "h"):
            for z in range(PASSES):
                wq[name, z] = quantize(name, z)
                for u in range(2):
                    product(name, wq[name, z], z, u)
        res["y"] = keep.tile([P, S], F32, name="y_rows", tag="e_stage1", align_bytes=64)
        for u in range(2):
            nc.vector.tensor_copy(res["y"][:, u * HALF : (u + 1) * HALF], banks["y", u][:])
        res["e"] = keep.tile([P, S], F32, name="e_rows", tag="h_wide0")
        res["h"] = keep.tile([P, S], F32, name="h_rows")
        for name in ("e", "h"):
            for u in range(2):
                nc.scalar.copy(res[name][:, u * HALF : (u + 1) * HALF], banks[name, u][:])

        yc = keep.tile([P, V], F32, name="yc", tag="h_stage0", align_bytes=64)
        nc.vector.tensor_copy(yc[:], res["y"][:].indirect(cen_t[:]))
        gate = []
        for d in range(3):
            pre = keep.tile([P, V], F32, name=f"pre{d}", tag=("h_stage1", "pre1", "pre2")[d], align_bytes=64)
            nc.vector.tensor_tensor(pre[:], res["e"][:].indirect(pos_t[d][:]), yc[:], ADD)
            g = keep.tile([P, V], F32, name=f"gate{d}")
            nc.scalar.activation(g[:], pre[:], SIGMOID)
            gate.append(g)
        term = [keep.tile([P, V], F32, name=f"term{d}") for d in range(3)]
        nc.vector.tensor_tensor(term[0][:], res["h"][:].indirect(pos_t[0][:]), gate[0][:], MULT)
        nc.vector.tensor_tensor(term[1][:], res["h"][:].indirect(pos_t[1][:]), gate[1][:], MULT)
        nc.vector.tensor_tensor(term[2][:], res["h"][:].indirect(pos_t[2][:]), gate[2][:], MULT)
        part = keep.tile([P, V], F32, name="part")
        nc.vector.tensor_tensor(part[:], term[0][:], term[1][:], ADD)
        total = keep.tile([P, V], F32, name="total")
        nc.vector.tensor_tensor(total[:], part[:], term[2][:], ADD)
        nc.sync.dma_start(out, total[:])
